import numpy as np, ml_dtypes
CORES = [3,11,19,27,35,43,51,59]
N = 8
import mx_ref
BF = ml_dtypes.bfloat16
def gcols(t, e):
    v = np.concatenate([t.reshape(8, 16, -1, 4), np.zeros((8, 16, 1, 4), BF)], axis=2)
    return np.ascontiguousarray(np.stack([v[g][:, e[g]] for g in range(8)])).reshape(128, -1)
def tile(rs):
    return np.stack(rs, axis=2).reshape(128, -1).astype(BF)
def pick(q, e):
    c = np.concatenate([q[0].reshape(128, -1, 4), np.zeros((128, 1, 4), np.uint8)], axis=1); s = np.concatenate([q[1], np.ones((16, 1), np.uint8)], axis=1)
    return (np.ascontiguousarray(c[:, e].reshape(128, -1)), np.ascontiguousarray(s[:, e]))
def join(*qs):
    return (np.concatenate([q[0] for q in qs], axis=1), np.concatenate([q[1] for q in qs], axis=1))
def put(q, e, v):
    c, s = q[0].reshape(128, -1, 4).copy(), q[1].copy(); c[:, e] = v[0].reshape(128, -1, 4); s[:, e] = v[1]
    return (c.reshape(128, -1), s)
def pk(c, s):
    return (np.ascontiguousarray(c), mx_ref.live(s))
def emit(q):
    return q[0], q[1]
def packed(v, rng):
    q = [mx_ref.quantize(np.ascontiguousarray(v[r])) for r in range(N)]
    return np.stack([a for a, b in q]), np.stack([mx_ref.plane(b, rng) for a, b in q])
def values_of_codes():
    e, c = np.zeros((128, 128, 4), np.float32), np.zeros((128, 2, 4), np.uint8)
    e[np.arange(128), np.arange(128), 0] = 1
    c[:127, :, 0] = np.arange(256).reshape(2, 128).T[:127]
    return mx_ref.matmul(mx_ref.quantize(e.reshape(128, 512).astype(BF)), (c.reshape(128, 8), np.full((16, 2), 127, np.uint8))).T.reshape(-1).astype(np.float64)
CODE_VALUE, SCALE_VALUE = values_of_codes(), 2.0 ** (np.arange(256) - 127.0)
def decode(q):
    return (CODE_VALUE[q[0]].reshape(16, 8, -1, 4) * SCALE_VALUE[q[1]][:, None, :, None] + 0.0).reshape(128, -1).astype(np.float32)
def f(rng, *shape):
    return mx_ref.flush((rng.standard_normal(shape, dtype=np.float32) * np.exp2(rng.integers(-2, 3, shape[:-1] + (1,)))).astype(BF))
def wide(rng, *shape, cols=0):
    v = rng.standard_normal(shape, dtype=np.float32) * np.exp2(rng.integers(-12, 13, shape)).astype(np.float32)
    if cols: v *= np.repeat(np.exp2(rng.integers(-cols, cols + 1, shape[:-2] + (1, shape[-1] // 4))) * (rng.random(shape[:-2] + (1, shape[-1] // 4)) > 0.0625), 4, axis=-1).astype(np.float32)
    return mx_ref.flush(v.astype(BF))
C, E = 384, 8
def big(v):
    v = v.astype(np.float32)
    v[np.abs(v) < np.float32(2.0 ** -16)] = 0
    return v.astype(BF)
def numbers_of(rng):
    return big(f(rng, N, 128, 4 * C)), big(f(rng, N, 128, 128)), np.array(f(rng, N, 128, 512)), np.array(f(rng, N, 128, 512))
def layers(rng):
    return big(f(rng, N, 128, 2048)).reshape(N, 8, 16, 4, 8, 16, 4)
def some(rng, k):
    return np.argsort(np.argsort(rng.random((8, 32)), axis=1), axis=1) < k
def flags(rng):
    k = np.where(some(rng, E // 2), -1.0, rng.random((N, 8, 32)))
    fl = np.ones((N, 8, 32), np.int32)
    np.put_along_axis(fl, np.argsort(k, axis=2)[:, :, :E], 0, axis=2)
    return fl
def relabels(rng):
    return np.argsort(rng.random((N, 7, 32, 32)), axis=3)
def drawn(rng, x, tr, u, v, fl, w, ti=None):
    t = tr.astype(np.float32).reshape(N, 8, 16, 32, 4).copy()
    t[np.broadcast_to((fl == 0)[:, :, None, :, None], t.shape)] = 0
    if ti is None: ti = relabels(rng)
    c, p = packed(np.ascontiguousarray(w).reshape(N, 128, 2048), rng)
    return {"x": np.ascontiguousarray(x).reshape(N, 128, 4 * C).astype(BF), "tr": t.reshape(N, 128, 128).astype(BF), "u": np.ascontiguousarray(u).reshape(N, 128, 512), "v": v, "fl": fl, "ti": ti.reshape(N, 7, 1024).astype(np.int32), "wc": c, "ws": p}
def setup_inputs(rng):
    x, tr, u, v = numbers_of(rng)
    return drawn(rng, x, tr, u, v, flags(rng), layers(rng))
def setup_inputs_ties(rng):
    x, tr, u, v = numbers_of(rng)
    o = rng.permutation(N)
    x = x.reshape(N, 8, 16, C, 4)
    for r in range(N):
        a = x[r][:, :8, :24].copy()
        a[:, :, 23] = 0
        k = rng.permutation(C) % 24
        if r == o[0]: k = np.zeros(C, int)
        if r == o[1]: k = np.full(C, 23)
        x[r][:, :8] = a[:, :, k]
    u = u.reshape(N, 8, 16, 128, 4)
    for i in range(5): u[:, :, 8:, i::16] = 0
    w = layers(rng)
    w[:, :, :, :, :, :8] = 0
    return drawn(rng, x, tr, u, v, flags(rng), w)
def setup_inputs_near(rng):
    x, tr, u, v = numbers_of(rng)
    fl, ti = flags(rng), relabels(rng)
    a = int(rng.integers(N))
    fl[(a + 1) % N] = fl[a]
    o = rng.permutation(N) % 2
    x = x.astype(np.float32).reshape(N, 8, 16, C, 4)
    tr = tr.astype(np.float32).reshape(N, 8, 16, 32, 4)
    x[:, :, :8] = 0
    tr[:, :, :8] = 0
    u = u.reshape(N, 128, 128, 4)
    for i in range(5): u[:, :, i::16] = 0
    for r in range(N):
        k = 2.0 ** -30 if o[r] == 0 else 1.0
        x[r, :, :5, :, 0] = k * rng.integers(-1, 2, (8, 5, C))
        tr[r, :, :5, :, 0] = k * rng.integers(-1, 2, (8, 5, 32))
        for g in rng.permutation(8)[:4]: x[r, g, :5, rng.integers(C), 0] = 2.0 ** 27 * rng.choice([-1.0, 1.0], 5)
        for h in range(0, 128, 16):
            for i in range(5): u[r, h + i, h + i, 0] = k
    hole = np.stack([np.flatnonzero(fl[a, g] == 0) for g in range(8)])
    held = np.stack([np.flatnonzero(fl[a, g] == 1) for g in range(8)])
    n = np.arange(8 * E)
    b = held[np.arange(8)[:, None], rng.integers(0, 32 - E, (8, 8 * E))]
    b[n // E, n] = hole[n // E, n % E]
    back = np.argsort(ti[a], axis=2)
    e = b.copy()
    for g in range(8):
        for h in range(g - 1, -1, -1): e[g] = back[h, b[h], e[g]]
    bit = (e[:, None] >> np.arange(4, -1, -1)[:, None]) & 1
    j = rng.permutation(C)[:8 * E]
    s = x[a, :, :5, :, 0]
    m = np.abs(s[:, :, j])
    s[:, :, j] = np.where(bit == 1, np.maximum(m, 2.0 ** -30 if o[a] == 0 else 1.0), 0.0 - m)
    x[a, :, :5, :, 0] = s
    w = layers(rng)
    w[:, :, :8] = 0
    w[:, :, :, :, :, :8] = 0
    return drawn(rng, x, tr, u, v, fl, w, ti)
def setup_inputs_deep(rng):
    x, tr, u, v = numbers_of(rng)
    x = (rng.integers(0, 2, x.shape) * 2.0 - 1.0) * (0.8 + 0.2 * rng.random(x.shape)) * 2.0 ** 26
    tr = (rng.integers(0, 2, tr.shape) * 2.0 - 1.0) * (0.8 + 0.2 * rng.random(tr.shape)) * 2.0 ** 26
    u = (rng.integers(0, 2, u.shape) * 2.0 - 1.0) * (0.9 + 0.1 * rng.random(u.shape)) * 2.0 ** 30
    o = rng.permutation(N)
    m = some(rng, E)
    fl = np.ones((N, 8, 32), np.int32)
    for r in range(N):
        if r == o[1]: fl[r, 7][m[7]] = 0
        elif r == o[2]: fl[r, 0][m[0]] = 0
        elif r != o[0]: fl[r][m] = 0
    w = (layers(rng).astype(np.float32) * np.float32(0.0625)).astype(BF)
    return drawn(rng, x.astype(np.float32), tr.astype(np.float32), u.astype(np.float32).astype(BF), v, fl, w)
def setup_inputs_odd(rng):
    x, tr, u, v = numbers_of(rng)
    x = (1.125 + 0.25 * rng.integers(0, 4, (N, 16, 8, C, 4))) * np.exp2(-rng.integers(8, 15, (N, 16, 8, C, 4)).astype(np.float32))
    x[:, :, 0, :, 0] = 1.96875
    x = x * (rng.integers(0, 2, x.shape) * 2.0 - 1.0) * np.exp2(rng.integers(-2, 3, (N, 16, 1, C, 1)).astype(np.float32))
    return drawn(rng, x.astype(np.float32), tr, u, v, flags(rng), layers(rng))
def setup_inputs_spread(rng):
    x, tr, u, v = numbers_of(rng)
    return drawn(rng, big(wide(rng, N, 128, 4 * C, cols=6)), big(wide(rng, N, 128, 128)), u, v, flags(rng), layers(rng))
def check_inputs(d):
    b = []
    for k in ("x", "tr", "u", "v"):
        a = np.abs(d[k].astype(np.float32))
        if not (np.isfinite(a).all() and ((a == 0) | (a >= 2.0 ** -30) & (a <= 2.0 ** 30)).all()): b.append("a value of " + k)
    fl = d["fl"]
    if not ((fl == 0) | (fl == 1)).all(): b.append("a flag of fl")
    if (np.sum(fl == 0, axis=2) > E).any(): b.append("too many empty slots in a level")
    if ((d["tr"].astype(np.float32).reshape(N, 8, 16, 32, 4) != 0) & (fl == 0)[:, :, None, :, None]).any(): b.append("tr isn't zero at an empty slot")
    if (np.sort(d["ti"].reshape(N, 7, 32, 32), axis=3) != np.arange(32)).any(): b.append("ti: not the points in some order")
    none, least, most = [emit(mx_ref.quantize(np.full((128, 16), k, np.float32).astype(BF)))[1][0, 0] for k in (0.0, 2.0 ** -30, 2.0 ** 30)]
    for r in range(N):
        if ((d["wc"][r] == 0x7F) | (d["wc"][r] == 0xFF)).any(): b.append("wc: a code that is no number")
        s = mx_ref.live(d["ws"][r])
        if ((s != none) & ((s < least) | (s > most))).any(): b.append("ws: a scale out of range")
    return b
def reference(x, tr, u, v, fl, ti, wc, ws):
    qu = [mx_ref.quantize(u[r]) for r in range(N)]
    lay = [pk(wc[r], ws[r]) for r in range(N)]
    now = [x[r] for r in range(N)]
    slot = [decode(mx_ref.quantize(tr[r])).astype(BF) for r in range(N)]
    full = fl > 0
    way = np.zeros((N, 8, C), np.int64)
    for t in range(3):
        claim, came = [], []
        for r in range(N):
            q = mx_ref.quantize(now[r])
            own = decode(q)
            s = mx_ref.matmul(qu[r], q)
            e = 16 * (s[0::16] > 0) + 8 * (s[1::16] > 0) + 4 * (s[2::16] > 0) + 2 * (s[3::16] > 0) + (s[4::16] > 0)
            fail = np.full(C, 8)
            for g in range(8):
                going = fail == 8
                way[r, g] = np.where(going, e[g], -1)
                fail = np.where(going & ~full[r, g][e[g]], g, fail)
                if g < 7: e[g + 1:] = ti[r, g][32 * e[g] + e[g + 1:]]
            passed = np.where(np.arange(8)[:, None] < fail, way[r], -1)
            z = (own - gcols(slot[r], passed).astype(np.float32)).astype(BF)
            q = mx_ref.quantize(z)
            c = np.full((8, 32), C)
            j = np.flatnonzero(fail < 8)
            np.minimum.at(c, (fail[j], way[r][fail[j], j]), j)
            claim.append(c < C)
            came.append(gcols(decode(q).astype(BF), np.where(c < C, c, -1)))
            now[r] = tile([mx_ref.matmul(pick(lay[r], np.arange(128 * b, 128 * b + 128)), q) * np.float32(0.015625) + z[:, b::4].astype(np.float32) for b in range(4)])
        for r in range(N):
            take = claim[(r - 1) % N] & ~full[r]
            slot[r] = gcols(np.concatenate([slot[r], came[(r - 1) % N]], axis=1), np.arange(32) + 32 * take)
            full[r] = full[r] | take
    y, bp, rt = np.zeros((N, 128, C), np.float32), np.zeros((N, 8, C + 32), np.float32), np.zeros((N, 128, 128), np.float32)
    oc, osc = np.zeros((N, 128, 4 * C), np.uint8), np.zeros((N, 16, C), np.uint8)
    for r in range(N):
        q = mx_ref.quantize(now[r])
        y[r] = mx_ref.matmul(mx_ref.quantize(v[r]), q)
        bp[r] = np.concatenate([way[r], full[r]], axis=1)
        rt[r] = slot[r].astype(np.float32)
        oc[r], osc[r] = emit(q)
    return {"y": y, "bp": bp, "rt": rt, "oc": oc, "osc": osc}

@@ -1,0 +1,491 @@
+import math
+from concourse.bass import DstId, RemoteDMATransfer
+from concourse.mybir import dt, AluOpType, AxisListType, ActivationFunctionType
+
+ROUNDS, C = 3, 384
+KIND = {"f": "float32", "b": "bfloat16", "i": "int32", "h": "uint16", "s": "uint8", "c": "float8_e4m3fn_x4"}
+SPEC = """b xt 1536 ut 512 vt 512 trt 512 et 2048 ent 2048 ct 512 bt 512 win 7168 tab 64 tat 64 res 1792 trb 1792 ow 768 lrow 512
+b ores 512 otr 512 fp 32 lf 32 gt 768 zt 1536 zp 1600 mw 256 mm 768 pr 768 jnk 384 lim 48 ctl 512 zero 512 lw 32 lw2 2 tw 2304
+b bw 128 qrow 256 otmp 256 obas 256
+c qxc 384 quc 128 qvc 128 qtc 128 wq 512 ec 512 enc 512 ctc 128 bc 128 qzc 384 qcc0 128 qcc1 128 qcc2 128 lc0 160 lc1 160 lc2 160
+s qxs 384 qus 128 qvs 128 qts 128 wp 512 es 512 ens 512 cts 128 bs 128 qzs 384 qcs0 128 qcs1 128 qcs2 128 ls0 160 ls1 160 ls2 160
+i tia 32 tib 32 pidx 1 pint 2 flw 2 flr 256
+h occ 32 lu 32 ol 24 clu 2 tl 4 tlf 4 of0 28 of1 28 of2 28 of3 28 of4 28 of5 28 of6 28
+f ones 128 idn 128 fs 768 cnt 2 emw 8 tk 2 tk2 2 rtt 128 yt 384 bpt 384 full 2 pf 2 hrow 7 s16 2 l16 2 i128 128 scl 8 w5 8 mh 8"""
+PSUM = ("ps", "pe", "pf0", "pf1", "pf2", "pf3", "pd0", "pd1")
+SCRATCH = {"tdr": ("dram", [160, 32], "bfloat16"), "fd0": ("dram", [2, 128, 2], "bfloat16"), "fd1": ("dram", [2, 128, 2], "bfloat16")}
+for _l in SPEC.split("\n"):
+    _w = _l.split()
+    for _k in range(1, len(_w), 2):
+        SCRATCH[_w[_k]] = ("sbuf", [128, int(_w[_k + 1])], KIND[_w[0]])
+for _n in PSUM:
+    SCRATCH[_n] = ("psum", [128, 512], "float32")
+DMAS = "dx du dti dtr dw dfl dflr dv dw0 dw1 dtd dw2 dw4 dl0 dl1 dl2 dlr0 dlr1 dlw0 dlw1 dout".split()
+SEMAPHORES = "cv ca ct_ cp loc rf0 rf1 rf2 rc0 rc1 rc2 rs0 rs1 rs2".split() + DMAS
+
+ADD, SUB, MUL, MAX, MIN = AluOpType.add, AluOpType.subtract, AluOpType.mult, AluOpType.max, AluOpType.min
+EQ, NE, GT, GE = AluOpType.is_equal, AluOpType.not_equal, AluOpType.is_gt, AluOpType.is_ge
+COPY = ActivationFunctionType.Copy
+
+
+def rank_program(g, core, T, topo):
+    rank = T.rank_of(core)
+    if rank is None:
+        return
+    nxt = T.cores[(rank + 1) % len(T.cores)]
+    eng = {"V": g.vector, "A": g.scalar, "T": g.tensor, "S": g.sync, "P": g}
+    semof = {"V": "cv", "A": "ca", "T": "ct_", "P": "cp"}
+    total = {}
+    known = {q: {} for q in eng}
+    clock = {}
+    wr, rd = {}, {}
+
+    def hit(a, b):
+        return a[0] < b[1] and b[0] < a[1] and a[2] < b[3] and b[2] < a[3] and (a[2] - b[2]) % math.gcd(a[4], b[4]) == 0
+
+    def covers(a, b):
+        return a[4] == 1 and a[0] <= b[0] and b[1] <= a[1] and a[2] <= b[2] and b[3] <= a[3]
+
+    def learn(q, sem, val):
+        k = known[q]
+        if k.get(sem, 0) >= val:
+            return
+        if sem in DMAS:
+            val = total[sem]
+        eng[q].wait_ge(T.sem[sem], val)
+        k[sem] = val
+        for (s, x), c in clock.items():
+            if s == sem and x <= val and (sem in DMAS or x == val):
+                for s2, x2 in c.items():
+                    if k.get(s2, 0) < x2:
+                        k[s2] = x2
+
+    def need(q, outs, ins):
+        toks = {}
+
+        def add(e):
+            toks[e[2]] = max(toks.get(e[2], 0), e[3])
+        for name, reg in ins:
+            for e in wr.get(name, []):
+                if hit(reg, e[0]):
+                    add(e)
+            if name in PSUM:
+                for e in rd.get(name, []):
+                    if e[1] != q:
+                        add(e)
+        for name, reg in outs:
+            for e in wr.get(name, []) + rd.get(name, []):
+                if name in PSUM or hit(reg, e[0]):
+                    add(e)
+        for s in sorted(toks):
+            learn(q, s, toks[s])
+
+    def note(q, outs, ins, sem, val):
+        for name, reg in outs:
+            wr[name] = [e for e in wr.get(name, []) if not covers(reg, e[0])] + [(reg, q, sem, val)]
+            rd[name] = [e for e in rd.get(name, []) if not covers(reg, e[0])]
+        for name, reg in ins:
+            rd.setdefault(name, []).append((reg, q, sem, val))
+
+    def regs(vs):
+        out = []
+        for e in vs:
+            out += e[1]
+        return out
+
+    def run(q, fn, outs, ins):
+        o, i = regs(outs), regs(ins)
+        need(q, o, i)
+        sem = semof[q]
+        total[sem] = total.get(sem, 0) + 1
+        clock[(sem, total[sem])] = dict(known[q])
+        fn().then_inc(T.sem[sem], 1)
+        note(q, o, i, sem, total[sem])
+
+    def dma(q, sem, out, in_):
+        o, i = regs([out]), regs([in_])
+        need(q, o, i)
+        total[sem] = total.get(sem, 0) + 16
+        clock[(sem, total[sem])] = dict(known[q])
+        eng[q].dma_start(out[0], in_[0]).then_inc(T.sem[sem], 16)
+        note(q, o, i, sem, total[sem])
+
+    def v(name, a, b, s=1, p=(0, 128)):
+        t = T[name]
+        return (t[p[0]:p[1], a:b:s] if s != 1 else t[p[0]:p[1], a:b], [(name, (p[0], p[1], a, b, s))])
+
+    def codes(name, a, b):
+        return (T[name][:, a:b].bitcast(dt.uint8), [(name, (0, 128, a, b, 1))])
+
+    def rows(name, a, b):
+        return (T[name][a:b, :], [(name, (a, b, 0, 32, 1))])
+
+    def inp(ap):
+        return (ap, [])
+
+    def ind(win, off):
+        return (win[0].indirect(off[0]), win[1] + off[1])
+
+    def copy(out, in_):
+        run("V", lambda: g.vector.tensor_copy(out[0], in_[0]), [out], [in_])
+
+    def act(out, in_, scale=1.0):
+        run("A", lambda: g.scalar.activation(out[0], in_[0], COPY, scale=scale) if scale != 1.0 else g.scalar.activation(out[0], in_[0], COPY), [out], [in_])
+
+    def tt(out, a, b, op):
+        run("V", lambda: g.vector.tensor_tensor(out[0], a[0], b[0], op), [out], [a, b])
+
+    def ts(out, a, s1, op0, s2=None, op1=None):
+        ins = [a] + [s for s in (s1, s2) if isinstance(s, tuple)]
+        x1 = s1[0] if isinstance(s1, tuple) else s1
+        x2 = s2[0] if isinstance(s2, tuple) else s2
+        if op1 is None:
+            run("V", lambda: g.vector.tensor_scalar(out[0], a[0], x1, None, op0), [out], ins)
+        else:
+            run("V", lambda: g.vector.tensor_scalar(out[0], a[0], x1, x2, op0, op1), [out], ins)
+
+    def fill(out, c):
+        run("V", lambda: g.vector.memset(out[0], c), [out], [])
+
+    def quant(c, s, in_):
+        run("V", lambda: g.vector.quantize_mx(c[0], s[0], in_[0]), [c, s], [in_])
+
+    def mx(out, lc, ls, rc, rs):
+        run("T", lambda: g.tensor.matmul_mx(out[0], lc[0], ls[0], rc[0], rs[0], True, True), [out], [lc, ls, rc, rs])
+
+    def pair(c, s, a, b):
+        return v(c, a, b), v(s, a, b)
+
+    def turn(out, in_):
+        run("V", lambda: g.vector.transpose(out[0], in_[0]), [out], [in_])
+
+    def iota(out, pattern, base, cm):
+        run("P", lambda: g.iota(out[0], pattern, base, cm, allow_small_or_imprecise_dtypes=True), [out], [])
+
+    def one(G, k=1):
+        return (16 * G, 16 * G + k)
+
+    dma("S", "dti", v("tia", 0, 32), inp(T.ti[0:4, :]))
+    dma("A", "dti", v("tib", 0, 32, p=(0, 96)), inp(T.ti[4:7, :]))
+    dma("S", "dx", v("xt", 0, 1536), inp(T.x[:]))
+    dma("A", "du", v("ut", 0, 512), inp(T.u[:]))
+
+    fill(v("ones", 0, 128), 1.0)
+    iota(v("pidx", 0, 1), [[0, 1]], 0, 1)
+    run("P", lambda: g.affine_select(T.idn[:], T.ones[:], [[-1, 128]], EQ, 0.0, 0, 1), [v("idn", 0, 128)], [v("ones", 0, 128)])
+    iota(v("hrow", 0, 7), [[1, 7]], 1, 0)
+    iota(v("s16", 0, 2), [[16, 2]], 0, 0)
+    iota(v("win", 0, 1024), [[1, 32], [0, 32]], 0, 0)
+    iota(v("win", 2048, 3072), [[0, 32], [1, 32]], 0, 0)
+    iota(v("win", 6144, 7168), [[0, 32], [1, 32]], 0, 0)
+    iota(v("flr", 0, 256), [[0, 256]], 1, 0)
+    iota(v("qrow", 0, 256), [[0, 8], [1, 16], [16, 2]], 0, 0)
+    iota(v("i128", 0, 128), [[1, 128]], -32, 0)
+    iota(v("bw", 0, 64), [[0, 2], [1, 2], [2, 16]], 0, 0)
+    fill(v("ent", 0, 2048), 0.0)
+    for b in range(4):
+        ts(v("ent", 512 * b + b, 512 * b + 512, 4), v("idn", 0, 128), -(2.0 ** -6), MUL)
+    fill(v("win", 1024, 2048), 0.0)
+    fill(v("ct", 0, 512), 0.0)
+    run("V", lambda: g.vector.tensor_scalar(T.pint[:, 0:1], T.pidx[:], 15, None, AluOpType.bitwise_and), [v("pint", 0, 1)], [v("pidx", 0, 1)])
+    run("V", lambda: g.vector.tensor_scalar(T.pint[:, 1:2], T.pidx[:], 4, None, AluOpType.arith_shift_right), [v("pint", 1, 2)], [v("pidx", 0, 1)])
+    copy(v("pf", 0, 2), v("pint", 0, 2))
+    i15, grp = v("pf", 0, 1), v("pf", 1, 2)
+    for k in range(5):
+        ts(v("w5", k, k + 1), i15, float(k), EQ, 2.0 ** (4 - k), MUL)
+    ts(v("w5", 6, 7), grp, 0.0, EQ, 32.0, MUL)
+    ts(v("scl", 0, 1), i15, 0.0, EQ)
+    ts(v("scl", 1, 2), i15, 1.0, EQ, 64.0, MUL)
+    run("V", lambda: g.vector.tensor_reduce(T.w5[:, 5:6], T.w5[:, 0:5], AxisListType.X, ADD), [v("w5", 5, 6)], [v("w5", 0, 5)])
+    wcol = v("w5", 5, 6)
+    fill(v("bt", 384, 512), 0.0)
+    fill(v("trt", 128, 512), 0.0)
+    tt(v("w5", 7, 8), v("w5", 6, 7), wcol, MUL)
+    ts(v("mh", 0, 7), v("hrow", 0, 7), grp, EQ, wcol, MUL)
+    ts(v("scl", 2, 3), v("scl", 0, 1), 32.0, MUL, v("scl", 1, 2), ADD)
+    ts(v("l16", 0, 2), v("s16", 0, 2), i15, ADD)
+    for k in range(4):
+        ts(v("ct", 5 * k, 112, 16), v("mh", 0, 7), v("w5", 7, 8), ADD)
+    copy(v("tab", 0, 32), v("tia", 0, 32))
+    copy(v("tab", 32, 64, p=(0, 96)), v("tib", 0, 32, p=(0, 96)))
+    turn(v("tat", 0, 32), v("tab", 0, 32))
+    turn(v("tat", 32, 64, p=(0, 96)), v("tab", 32, 64, p=(0, 96)))
+    act(v("win", 3072, 4096), v("ent", 0, 1024), 0.0)
+    for G in range(6):
+        dma("SA"[G % 2], "dw0", v("win", 0, 1024, p=one(G)), v("tab", 0, 32, p=(0, 32)))
+    dma("S", "dtd", rows("tdr", 0, 64), v("tat", 0, 32, p=(64, 128)))
+    dma("A", "dtd", rows("tdr", 64, 160), v("tat", 32, 64, p=(0, 96)))
+    for G in range(6):
+        dma("SA"[G % 2], "dw1", v("win", 1024, 2048, p=one(G)), v("tat", 0, 32, p=(32, 64)))
+    act(v("win", 5120, 6144), v("ent", 0, 1024), 0.0)
+    act(v("win", 4096, 5120), v("win", 2048, 3072))
+    act(v("et", 0, 2048), v("ent", 0, 2048), -1.0)
+    act(v("tw", 0, 2048), v("ent", 0, 2048), 0.0)
+    act(v("tw", 2048, 2304), v("ent", 0, 256), 0.0)
+    dma("S", "dtr", v("trt", 0, 128), inp(T.tr[:]))
+    for G in range(6):
+        dma("S", "dw2", v("win", 2048, 4096, p=one(G)), rows("tdr", 0, 64))
+    dma("S", "dfl", v("flw", 0, 2), inp(T.fl[:]))
+    for G in range(6):
+        dma("S", "dw4", v("win", 4096, 7168, p=one(G)), rows("tdr", 64, 160))
+    for G in range(6):
+        for k in range(2):
+            dma("S", "dflr", v("flr", 0, 256, p=(16 * G + k, 16 * G + k + 1)), inp(T.fl[:]))
+    dma("S", "dw", codes("wq", 0, 512), inp(T.wc[:]))
+    dma("S", "dw", v("wp", 0, 512), inp(T.ws[:]))
+    dma("S", "dv", v("vt", 0, 512), inp(T.v[:]))
+    quant(*pair("ctc", "cts", 0, 128), v("ct", 0, 512))
+    ts(v("scl", 3, 4), v("scl", 2, 3), -1.0, MUL)
+    quant(*pair("quc", "qus", 0, 128), v("ut", 0, 512))
+
+    def first_rest():
+        for s in range(2):
+            ts(v("mw", 128 * s, 128 * s + 128), v("i128", 0, 128), v("l16", s, s + 1), NE)
+        fill(v("bw", 64, 128), -1.0)
+        for t in range(4):
+            fill(v("zp", 400 * t + 384, 400 * t + 400), 0.0)
+        fill(v("ctl", 128, 512), 0.0)
+        fill(v("lrow", 0, 512), 128.0)
+        fill(v("zero", 0, 512), 0.0)
+        for k in range(3):
+            quant(*pair("lc%d" % k, "ls%d" % k, 32, 160), v("zero", 0, 512))
+        ts(v("emw", 0, 2), v("flw", 0, 2), -128.0, MUL, 128.0, ADD)
+
+    elist = topo.engines(core, nxt)
+    n = 1
+    while n * 2 <= len(elist) and n < 8:
+        n *= 2
+    elist = elist[:n]
+    full_mask = sum(1 << e for e in elist)
+    half = len(elist) // 2
+    halves = [sum(1 << e for e in elist[:half]), sum(1 << e for e in elist[half:])]
+    rid, pid, _ = topo.addr(nxt)
+
+    def send(ins, cnt, fn):
+        need("P", [], regs(ins))
+        total["loc"] = total.get("loc", 0) + cnt
+        fn()
+        note("P", [], regs(ins), "loc", total["loc"])
+
+    def arrived(where, sem):
+        total[sem] = n
+        note("R", where, [], sem, n)
+
+    def flags_out(r):
+        k, sem = 16 * r, "rf%d" % r
+        if r == ROUNDS - 1:
+            send([v("lim", k + 2, k + 4)], n, lambda: g.remote_dma(T.lw2[:], T.lim[:, k + 2:k + 4], T.sem[sem], T.sem.loc, pid, rid, full_mask))
+            arrived([("lw2", (0, 128, 0, 2, 1))], sem)
+        else:
+            fd = T["fd%d" % r]
+            tr = [RemoteDMATransfer(dst_ids=[DstId(rid=rid, pnc=pid)], dma_engine_mask=halves[e], remote_sem=T.sem[sem], src=T.lim[:, k + 2 * e:k + 2 * e + 2], dst=fd[e]) for e in range(2)]
+            send([v("lim", k, k + 4)], n, lambda: g.remote_dma_fused(tr, local_sem=T.sem.loc))
+            arrived([("fd%d" % r, (0, 2, 0, 256, 1))], sem)
+
+    def claims_out(r):
+        lc, ls, qc, qs = T["lc%d" % r], T["ls%d" % r], T["qcc%d" % r], T["qcs%d" % r]
+        send([v("qcc%d" % r, 0, 32)], n, lambda: g.remote_dma(lc[:, 0:32].bitcast(dt.uint8), qc[:, 0:32].bitcast(dt.uint8), T.sem["rc%d" % r], T.sem.loc, pid, rid, full_mask))
+        send([v("qcs%d" % r, 0, 32)], n, lambda: g.remote_dma(ls[:, 0:32], qs[:, 0:32], T.sem["rs%d" % r], T.sem.loc, pid, rid, full_mask))
+        arrived([("lc%d" % r, (0, 128, 0, 32, 1))], "rc%d" % r)
+        arrived([("ls%d" % r, (0, 128, 0, 32, 1))], "rs%d" % r)
+
+    def flags_in(r):
+        fd = (T["fd%d" % r][:], [("fd%d" % r, (0, 2, 0, 256, 1))])
+        for G in range(6):
+            dma("S", "dlr%d" % r, v("lrow", 256 * r, 256 * r + 256, p=one(G, 2)), fd)
+        dma("S", "dlw%d" % r, v("lw", 16 * r, 16 * r + 2), (T["fd%d" % r][1], fd[1]))
+
+    def take_list(r):
+        src = v("lw2", 0, 2) if r == ROUNDS - 1 else v("lw", 16 * r, 16 * r + 2)
+        tt(v("emw", 2 * r + 2, 2 * r + 4), v("emw", 2 * r, 2 * r + 2), src, MIN)
+        tt(v("tk", 0, 2), v("emw", 2 * r, 2 * r + 2), v("emw", 2 * r + 2, 2 * r + 4), SUB)
+        tt(v("tk2", 0, 2), v("tk", 0, 2), v("l16", 0, 2), ADD)
+        if r == ROUNDS - 1:
+            copy(v("tlf", 0, 4, 2), v("tk2", 0, 2))
+        else:
+            copy(v("tl", 2 * r, 2 * r + 2), v("tk2", 0, 2))
+
+    def unpack(r):
+        for t in range(4):
+            pd = "pd%d" % (t % 2)
+            mx(v(pd, 0, 128), *pair("enc", "ens", 128 * t, 128 * t + 128), *pair("lc%d" % r, "ls%d" % r, 0, 128))
+            a = 768 * r + 192 * t + 128
+            if t % 2 and r == ROUNDS - 1:
+                copy(v("tw", a, a + 32), v(pd, 0, 32))
+            else:
+                act(v("tw", a, a + 32), v(pd, 0, 32))
+
+    def new_slots(r):
+        for t in range(4):
+            a = 768 * r + 192 * t
+            act(v("tw", a + 768, a + 800), ind(v("tw", a, a + 160), v("tl", 2 * r, 2 * r + 2)))
+
+    def lists(r):
+        k = 16 * r
+        copy(v("clu", 0, 2), v("cnt", 0, 2))
+        ts(v("lim", k + 2, k + 4), v("cnt", 0, 2), float(C), GE, 128.0, MUL)
+        if r < ROUNDS - 1:
+            tt(v("lim", k, k + 2), v("lim", k + 2, k + 4), v("l16", 0, 2), ADD)
+        flags_out(r)
+        for t in range(4):
+            act(v("ctl", t, 128, 4), ind(v("zp", 400 * t, 400 * t + 400), v("clu", 0, 2)))
+
+    def pack(r):
+        quant(*pair("qcc%d" % r, "qcs%d" % r, 0, 128), v("ctl", 0, 512))
+        claims_out(r)
+
+    LO = [0]
+    for h in range(7):
+        LO.append(LO[h] + 64 * (7 - h))
+    qx = pair("qxc", "qxs", 0, 384)
+    for r in range(ROUNDS):
+        last = r == ROUNDS - 1
+        quant(*qx, v("xt", 0, 1536))
+        mx(v("ps", 0, 384), *pair("quc", "qus", 0, 128), *qx)
+        if r > 0:
+            mx(v("pf0", 0, 384), *pair("ec", "es", 0, 128), *qx)
+            lists(r - 1)
+        else:
+            quant(*pair("enc", "ens", 0, 512), v("ent", 0, 2048))
+        for x in range(16):
+            ts(v("bt", 24 * x, 24 * x + 24), v("ps", x, 384, 16), 0.0, GT)
+        quant(*pair("bc", "bs", 0, 128), v("bt", 0, 512))
+        mx(v("pe", 0, 128), *pair("bc", "bs", 0, 128), *pair("ctc", "cts", 0, 128))
+        if r == 0:
+            quant(*pair("ec", "es", 0, 512), v("et", 0, 2048))
+            mx(v("pf0", 0, 384), *pair("ec", "es", 0, 128), *qx)
+        else:
+            pack(r - 1)
+            flags_in(r - 1)
+        for b in range(1, 4):
+            mx(v("pf%d" % b, 0, 384), *pair("ec", "es", 128 * b, 128 * b + 128), *qx)
+        for b in range(2):
+            act(v("fs", 384 * b, 384 * b + 384), v("pf%d" % b, 0, 384))
+        copy(v("of0", 0, 28), v("pe", 0, 28))
+        for h in range(7):
+            a, m = LO[h], 7 - h
+            copy(v("res", a, a + 64 * m), ind(v("win", 1024 * h, 1024 * h + 1024), v("of%d" % h, 0, 4 * m)))
+            if r == 0 and h == 1:
+                fill(v("fp", 0, 4), 0.0)
+                quant(*pair("qtc", "qts", 0, 128), v("trt", 0, 512))
+            if r == 0 and h == 2:
+                ts(v("obas", 0, 256), v("qrow", 0, 256), v("scl", 0, 1), MUL)
+            if r == 0 and h == 3:
+                ts(v("otmp", 0, 256), v("flr", 0, 256), v("scl", 3, 4), MUL, v("scl", 2, 3), ADD)
+            if h == 5:
+                if r == 0:
+                    tt(v("ow", 0, 256), v("otmp", 0, 256), v("obas", 0, 256), ADD)
+                else:
+                    tt(v("ow", 256 * r, 256 * r + 256), v("ow", 256 * r - 256, 256 * r), v("lrow", 256 * r - 256, 256 * r), MIN)
+                act(v("ores", 0, 384), ind(v("ow", 256 * r, 256 * r + 256), v("occ", 0, 24)))
+            if h == 6:
+                for k in range(4):
+                    e = v("otr", 16 * k + 1, 384, 64)
+                    run("V", lambda: g.vector.tensor_tensor_scan(T.fp[:, 4 + k:28:4], e[0], e[0], 0.0, MAX, MAX), [v("fp", 4 + k, 28, 4)], [e])
+            turn(v("trb", a, a + 64 * m), v("res", a, a + 64 * m))
+            if h < 6:
+                for k in range(4):
+                    ts(v("of%d" % (h + 1), k, 4 * (m - 1), 4), v("trb", a + 64 + 16 * k, a + 64 * m, 64), 32.0, MUL, v("trb", a + 16 * k, a + 16 * k + 1), ADD)
+            if h == 6:
+                tt(v("lf", 0, 24), v("otr", 0, 384, 16), v("fp", 0, 24), ADD)
+            if h % 2 == 0:
+                ts(v("occ", 4 * h, 4 * h + 4), v("trb", a + 1, a + 64, 16), 32.0 * h, ADD)
+                ts(v("occ", 4 * h + 4, 4 * h + 8), v("trb", a, a + 64, 16), 32.0 * h + 32.0, ADD)
+            if h == 5:
+                turn(v("otr", 0, 384), v("ores", 0, 384))
+        copy(v("lu", 0, 24), v("lf", 0, 24))
+        dl = "dl%d" % r
+        for lev in range(6):
+            dma("S", dl, v("ol", 0, 24, p=one(lev, 16)), v("lu", 4 * lev, 4 * lev + 4, p=(0, 96)))
+        if r == 0:
+            for t in range(4):
+                pd = "pd%d" % (t % 2)
+                mx(v(pd, 0, 128), *pair("enc", "ens", 128 * t, 128 * t + 128), *pair("qtc", "qts", 0, 128))
+                for s in range(2):
+                    act(v("tw", 192 * t + 16 * s, 192 * t + 16 * s + 16), v(pd, s, 32, 2))
+        copy(v("ores", 384, 512), ind(v("ow", 256 * r, 256 * r + 256), v("occ", 24, 32)))
+        turn(v("otr", 384, 512), v("ores", 384, 512))
+        tt(v("fp", 28, 32), v("fp", 24, 28), v("otr", 385, 448, 16), MAX)
+        tt(v("lf", 24, 32), v("otr", 384, 512, 16), v("fp", 24, 32), ADD)
+        copy(v("lu", 24, 32), v("lf", 24, 32))
+        dma("S", dl, v("ol", 0, 24, p=one(6, 16)), v("lu", 24, 28, p=(0, 96)))
+        dma("A", dl, v("ol", 0, 24, p=one(7, 16)), v("lu", 28, 32, p=(0, 96)))
+        if r == 0:
+            first_rest()
+        else:
+            unpack(r - 1)
+            take_list(r - 1)
+            new_slots(r - 1)
+        if last:
+            quant(*pair("qvc", "qvs", 0, 128), v("vt", 0, 512))
+        ol = v("ol", 0, 24)
+        for t in range(2, 4):
+            a = 768 * r + 192 * t
+            act(v("gt", 384 * (t - 2), 384 * (t - 1)), ind(v("tw", a, a + 128), ol))
+        for t in range(4):
+            a = 768 * r + 192 * t
+            if t < 2:
+                tt(v("zt", t, 1536, 4), ind(v("tw", a, a + 128), ol), v("fs", 384 * t, 384 * t + 384), ADD)
+            else:
+                tt(v("zt", t, 1536, 4), v("pf%d" % t, 0, 384), v("gt", 384 * (t - 2), 384 * (t - 1)), ADD)
+        quant(*pair("qzc", "qzs", 0, 384), v("zt", 0, 1536))
+        for s in range(2):
+            act(v("mm", 384 * s, 384 * s + 384), ind(v("mw", 128 * s, 128 * s + 128), ol))
+        for t in range(4):
+            mx(v("pf%d" % t, 0, 384), *pair("wq", "wp", 128 * t, 128 * t + 128), *pair("qzc", "qzs", 0, 384))
+        for t in range(4):
+            if t < 2:
+                ts(v("zp", 400 * t, 400 * t + 384), v("zt", t, 1536, 4), 64.0, MUL)
+            else:
+                act(v("zp", 400 * t, 400 * t + 384), v("zt", t, 1536, 4), 64.0)
+
+        def first_of(s):
+            e = v("mm", 384 * s, 384 * s + 384)
+            o = v("pr", 384 * s, 384 * s + 384)
+            run("V", lambda: g.vector.tensor_tensor_scan(o[0], e[0], e[0], 1.0, MUL, MIN), [o], [e])
+            if last:
+                run("V", lambda: g.vector.tensor_reduce(T.cnt[:, s:s + 1], o[0], AxisListType.X, ADD), [v("cnt", s, s + 1)], [o])
+            else:
+                run("A", lambda: g.scalar.activation(T.jnk[:], o[0], COPY, accum_out=T.cnt[:, s:s + 1]), [v("jnk", 0, 384), v("cnt", s, s + 1)], [o])
+
+        def layer(t):
+            tt(v("xt", t, 1536, 4), v("pf%d" % t, 0, 384), v("zp", 400 * t, 400 * t + 384), ADD)
+        first_of(0)
+        if last:
+            first_of(1)
+            lists(r)
+            layer(0)
+            layer(1)
+            pack(r)
+        else:
+            layer(0)
+            first_of(1)
+            layer(1)
+        layer(2)
+        layer(3)
+    r = ROUNDS - 1
+    quant(*qx, v("xt", 0, 1536))
+    mx(v("ps", 0, 384), *pair("qvc", "qvs", 0, 128), *qx)
+    dma("S", "dout", inp(T.oc[:]), codes("qxc", 0, 384))
+    for k in range(4):
+        dma("S", "dout", inp(T.osc[4 * k:4 * k + 4, :]), v("qxs", 0, 384, p=(32 * k, 32 * k + 4)))
+    act(v("bpt", 0, 384), ind(v("bw", 0, 128), v("ol", 0, 24)))
+    dma("S", "dout", inp(T.bp[:, 0:384]), (T.bpt[0:128:16, :], [("bpt", (0, 128, 0, 384, 1))]))
+    copy(v("yt", 0, 384), v("ps", 0, 384))
+    dma("S", "dout", inp(T.y[:]), v("yt", 0, 384))
+    take_list(r)
+    ts(v("full", 0, 2), v("emw", 2 * r + 2, 2 * r + 4), 0.0, EQ)
+    dma("S", "dout", inp(T.bp[:, 384:416]), v("full", 0, 2))
+    unpack(r)
+    for t in range(4):
+        a = 768 * r + 192 * t
+        for s in range(2):
+            out, win = v("rtt", 4 * s + t, 128, 8), ind(v("tw", a, a + 160), v("tlf", 2 * s, 2 * s + 1))
+            if t % 2:
+                ts(out, win, -64.0, MUL)
+            else:
+                act(out, win, -64.0)
+    dma("S", "dout", inp(T.rt[:]), v("rtt", 0, 128))
+    for s in sorted(total):
+        if known["P"].get(s, 0) < total[s]:
+            g.wait_ge(T.sem[s], total[s])

@@ -3,25 +3,28 @@ from concourse.bass import DstId, RemoteDMATransfer
 from concourse.mybir import dt, AluOpType, AxisListType, ActivationFunctionType
 
 ROUNDS, C = 3, 384
+SHARE, FSL, NZ = (3, 3, 2, 2, 1, 1, 0), (3, 4), 1
 KIND = {"f": "float32", "b": "bfloat16", "i": "int32", "h": "uint16", "s": "uint8", "c": "float8_e4m3fn_x4"}
-SPEC = """b xt 1536 ut 512 vt 512 trt 512 et 2048 ent 2048 ct 512 bt 512 win 7168 tab 64 tat 64 res 1792 trb 1792 ow 768 lrow 512
-b ores 512 otr 512 fp 32 lf 32 gt 768 zt 1536 zp 1600 mw 256 mm 768 pr 768 jnk 384 lim 48 ctl 512 zero 512 lw 32 lw2 2 tw 2304
-b bw 128 qrow 256 otmp 256 obas 256
+SPEC = """b xt 1536 ut 512 vt 512 trt 512 et 2048 ent 2048 ct 512 bt 512 win 7168 tab 64 tat 64 res 1792 trb 1792 ow 768
+b ores 512 otr 512 fp 32 lf 32 gt 768 zt 1536 zp 1600 mw 256 mm 768 pr 768 jnk 384 lim 64 ctl 512 zero 512 lw 64 tw 2304
+b bw 128 me 4 nx 4
 c qxc 384 quc 128 qvc 128 qtc 128 wq 512 ec 512 enc 512 ctc 128 bc 128 qzc 384 qcc0 128 qcc1 128 qcc2 128 lc0 160 lc1 160 lc2 160
 s qxs 384 qus 128 qvs 128 qts 128 wp 512 es 512 ens 512 cts 128 bs 128 qzs 384 qcs0 128 qcs1 128 qcs2 128 ls0 160 ls1 160 ls2 160
-i tia 32 tib 32 pidx 1 pint 2 flw 2 flr 256
+i tia 32 tib 32 pidx 1 pint 2 flw 2
 h occ 32 lu 32 ol 24 clu 2 tl 4 tlf 4 of0 28 of1 28 of2 28 of3 28 of4 28 of5 28 of6 28
-f ones 128 idn 128 fs 768 cnt 2 emw 8 tk 2 tk2 2 rtt 128 yt 384 bpt 384 full 2 pf 2 hrow 7 s16 2 l16 2 i128 128 scl 8 w5 8 mh 8"""
+f ones 128 idn 128 fs 768 cnt 2 tk 2 rtt 128 yt 384 bpt 384 full 2 pf 2 hrow 7 s16 2 l16 2 i128 128 w5 8 mh 8"""
 PSUM = ("ps", "pe", "pf0", "pf1", "pf2", "pf3", "pd0", "pd1")
-SCRATCH = {"tdr": ("dram", [160, 32], "bfloat16"), "fd0": ("dram", [2, 128, 2], "bfloat16"), "fd1": ("dram", [2, 128, 2], "bfloat16")}
+SCRATCH = {"tdr": ("dram", [160, 32], "bfloat16")}
+for _n in ("fo", "fd0", "fd1"):
+    SCRATCH[_n] = ("dram", [2, 128, 2], "bfloat16")
 for _l in SPEC.split("\n"):
     _w = _l.split()
     for _k in range(1, len(_w), 2):
         SCRATCH[_w[_k]] = ("sbuf", [128, int(_w[_k + 1])], KIND[_w[0]])
 for _n in PSUM:
     SCRATCH[_n] = ("psum", [128, 512], "float32")
-DMAS = "dx du dti dtr dw dfl dflr dv dw0 dw1 dtd dw2 dw4 dl0 dl1 dl2 dlr0 dlr1 dlw0 dlw1 dout".split()
-SEMAPHORES = "cv ca ct_ cp loc rf0 rf1 rf2 rc0 rc1 rc2 rs0 rs1 rs2".split() + DMAS
+DMAS = "dx du dti dtr dw dfl dfo dow0 dv dw0 dw1 dtd dw2 dw4 dl0 dl1 dl2 dlr0 dlr1 dlw0 dlw1 dout".split()
+SEMAPHORES = "cv ca ct_ cp loc rn rf0 rf1 rf2 rc0 rc1 rc2 rs0 rs1 rs2".split() + DMAS
 
 ADD, SUB, MUL, MAX, MIN = AluOpType.add, AluOpType.subtract, AluOpType.mult, AluOpType.max, AluOpType.min
 EQ, NE, GT, GE = AluOpType.is_equal, AluOpType.not_equal, AluOpType.is_gt, AluOpType.is_ge
@@ -32,7 +35,7 @@ def rank_program(g, core, T, topo):
     rank = T.rank_of(core)
     if rank is None:
         return
-    nxt = T.cores[(rank + 1) % len(T.cores)]
+    nxt, prv = T.cores[(rank + 1) % len(T.cores)], T.cores[(rank - 1) % len(T.cores)]
     eng = {"V": g.vector, "A": g.scalar, "T": g.tensor, "S": g.sync, "P": g}
     semof = {"V": "cv", "A": "ca", "T": "ct_", "P": "cp"}
     total = {}
@@ -120,6 +123,9 @@ def rank_program(g, core, T, topo):
     def rows(name, a, b):
         return (T[name][a:b, :], [(name, (a, b, 0, 32, 1))])
 
+    def slot(name, k=None):
+        return (T[name][:], [(name, (0, 2, 0, 256, 1))]) if k is None else (T[name][k], [(name, (k, k + 1, 0, 256, 1))])
+
     def inp(ap):
         return (ap, [])
 
@@ -169,6 +175,8 @@ def rank_program(g, core, T, topo):
     dma("A", "dti", v("tib", 0, 32, p=(0, 96)), inp(T.ti[4:7, :]))
     dma("S", "dx", v("xt", 0, 1536), inp(T.x[:]))
     dma("A", "du", v("ut", 0, 512), inp(T.u[:]))
+    dma("S", "dtr", v("trt", 0, 128), inp(T.tr[:]))
+    dma("S", "dfl", v("flw", 0, 2), inp(T.fl[:]))
 
     fill(v("ones", 0, 128), 1.0)
     iota(v("pidx", 0, 1), [[0, 1]], 0, 1)
@@ -178,9 +186,9 @@ def rank_program(g, core, T, topo):
     iota(v("win", 0, 1024), [[1, 32], [0, 32]], 0, 0)
     iota(v("win", 2048, 3072), [[0, 32], [1, 32]], 0, 0)
     iota(v("win", 6144, 7168), [[0, 32], [1, 32]], 0, 0)
-    iota(v("flr", 0, 256), [[0, 256]], 1, 0)
-    iota(v("qrow", 0, 256), [[0, 8], [1, 16], [16, 2]], 0, 0)
     iota(v("i128", 0, 128), [[1, 128]], -32, 0)
+    iota(v("ow", 0, 768), [[0, 768]], 0, 0)
+    iota(v("tw", 0, 2304), [[0, 2304]], 0, 0)
     iota(v("bw", 0, 64), [[0, 2], [1, 2], [2, 16]], 0, 0)
     fill(v("ent", 0, 2048), 0.0)
     for b in range(4):
@@ -194,15 +202,12 @@ def rank_program(g, core, T, topo):
     for k in range(5):
         ts(v("w5", k, k + 1), i15, float(k), EQ, 2.0 ** (4 - k), MUL)
     ts(v("w5", 6, 7), grp, 0.0, EQ, 32.0, MUL)
-    ts(v("scl", 0, 1), i15, 0.0, EQ)
-    ts(v("scl", 1, 2), i15, 1.0, EQ, 64.0, MUL)
     run("V", lambda: g.vector.tensor_reduce(T.w5[:, 5:6], T.w5[:, 0:5], AxisListType.X, ADD), [v("w5", 5, 6)], [v("w5", 0, 5)])
     wcol = v("w5", 5, 6)
     fill(v("bt", 384, 512), 0.0)
     fill(v("trt", 128, 512), 0.0)
     tt(v("w5", 7, 8), v("w5", 6, 7), wcol, MUL)
     ts(v("mh", 0, 7), v("hrow", 0, 7), grp, EQ, wcol, MUL)
-    ts(v("scl", 2, 3), v("scl", 0, 1), 32.0, MUL, v("scl", 1, 2), ADD)
     ts(v("l16", 0, 2), v("s16", 0, 2), i15, ADD)
     for k in range(4):
         ts(v("ct", 5 * k, 112, 16), v("mh", 0, 7), v("w5", 7, 8), ADD)
@@ -220,23 +225,25 @@ def rank_program(g, core, T, topo):
     act(v("win", 5120, 6144), v("ent", 0, 1024), 0.0)
     act(v("win", 4096, 5120), v("win", 2048, 3072))
     act(v("et", 0, 2048), v("ent", 0, 2048), -1.0)
-    act(v("tw", 0, 2048), v("ent", 0, 2048), 0.0)
-    act(v("tw", 2048, 2304), v("ent", 0, 256), 0.0)
-    dma("S", "dtr", v("trt", 0, 128), inp(T.tr[:]))
     for G in range(6):
         dma("S", "dw2", v("win", 2048, 4096, p=one(G)), rows("tdr", 0, 64))
-    dma("S", "dfl", v("flw", 0, 2), inp(T.fl[:]))
     for G in range(6):
         dma("S", "dw4", v("win", 4096, 7168, p=one(G)), rows("tdr", 64, 160))
-    for G in range(6):
-        for k in range(2):
-            dma("S", "dflr", v("flr", 0, 256, p=(16 * G + k, 16 * G + k + 1)), inp(T.fl[:]))
     dma("S", "dw", codes("wq", 0, 512), inp(T.wc[:]))
     dma("S", "dw", v("wp", 0, 512), inp(T.ws[:]))
     dma("S", "dv", v("vt", 0, 512), inp(T.v[:]))
     quant(*pair("ctc", "cts", 0, 128), v("ct", 0, 512))
-    ts(v("scl", 3, 4), v("scl", 2, 3), -1.0, MUL)
     quant(*pair("quc", "qus", 0, 128), v("ut", 0, 512))
+
+    def slots_first():
+        ts(v("me", 2, 4), v("flw", 0, 2), -64.0, MUL, 64.0, ADD)
+        ts(v("tk", 0, 2), v("flw", 0, 2), -32.0, MUL, 32.0, ADD)
+        tt(v("me", 0, 2), v("tk", 0, 2), v("l16", 0, 2), ADD)
+        for k in range(2):
+            dma("S", "dfo", slot("fo", k), v("me", 2 * k, 2 * k + 2))
+        for G in range(6):
+            dma("S", "dow0", v("ow", 0, 256, p=one(G, 2)), slot("fo"))
+        copy(v("lw", 0, 2), v("me", 2, 4))
 
     def first_rest():
         for s in range(2):
@@ -245,11 +252,9 @@ def rank_program(g, core, T, topo):
         for t in range(4):
             fill(v("zp", 400 * t + 384, 400 * t + 400), 0.0)
         fill(v("ctl", 128, 512), 0.0)
-        fill(v("lrow", 0, 512), 128.0)
         fill(v("zero", 0, 512), 0.0)
         for k in range(3):
             quant(*pair("lc%d" % k, "ls%d" % k, 32, 160), v("zero", 0, 512))
-        ts(v("emw", 0, 2), v("flw", 0, 2), -128.0, MUL, 128.0, ADD)
 
     elist = topo.engines(core, nxt)
     n = 1
@@ -267,15 +272,21 @@ def rank_program(g, core, T, topo):
         fn()
         note("P", [], regs(ins), "loc", total["loc"])
 
-    def arrived(where, sem):
-        total[sem] = n
-        note("R", where, [], sem, n)
+    def arrived(where, sem, cnt=n):
+        total[sem] = cnt
+        note("R", where, [], sem, cnt)
+
+    def tell():
+        ridb, pidb, _b = topo.addr(prv)
+        maskb = sum(1 << e for e in topo.engines(core, prv)[:half])
+        send([v("me", 0, 4)], half, lambda: g.remote_dma(T.nx[:], T.me[:], T.sem.rn, T.sem.loc, pidb, ridb, maskb))
+        arrived([("nx", (0, 128, 0, 4, 1))], "rn", half)
 
     def flags_out(r):
         k, sem = 16 * r, "rf%d" % r
         if r == ROUNDS - 1:
-            send([v("lim", k + 2, k + 4)], n, lambda: g.remote_dma(T.lw2[:], T.lim[:, k + 2:k + 4], T.sem[sem], T.sem.loc, pid, rid, full_mask))
-            arrived([("lw2", (0, 128, 0, 2, 1))], sem)
+            send([v("lim", k + 2, k + 4)], n, lambda: g.remote_dma(T.lw[:, k + 16:k + 18], T.lim[:, k + 2:k + 4], T.sem[sem], T.sem.loc, pid, rid, full_mask))
+            arrived([("lw", (0, 128, k + 16, k + 18, 1))], sem)
         else:
             fd = T["fd%d" % r]
             tr = [RemoteDMATransfer(dst_ids=[DstId(rid=rid, pnc=pid)], dma_engine_mask=halves[e], remote_sem=T.sem[sem], src=T.lim[:, k + 2 * e:k + 2 * e + 2], dst=fd[e]) for e in range(2)]
@@ -290,20 +301,16 @@ def rank_program(g, core, T, topo):
         arrived([("ls%d" % r, (0, 128, 0, 32, 1))], "rs%d" % r)
 
     def flags_in(r):
-        fd = (T["fd%d" % r][:], [("fd%d" % r, (0, 2, 0, 256, 1))])
         for G in range(6):
-            dma("S", "dlr%d" % r, v("lrow", 256 * r, 256 * r + 256, p=one(G, 2)), fd)
-        dma("S", "dlw%d" % r, v("lw", 16 * r, 16 * r + 2), (T["fd%d" % r][1], fd[1]))
+            dma("S", "dlr%d" % r, v("ow", 256 * r + 256, 256 * r + 512, p=one(G, 2)), slot("fd%d" % r))
+        dma("S", "dlw%d" % r, v("lw", 16 * r + 16, 16 * r + 18), slot("fd%d" % r, 1))
 
     def take_list(r):
-        src = v("lw2", 0, 2) if r == ROUNDS - 1 else v("lw", 16 * r, 16 * r + 2)
-        tt(v("emw", 2 * r + 2, 2 * r + 4), v("emw", 2 * r, 2 * r + 2), src, MIN)
-        tt(v("tk", 0, 2), v("emw", 2 * r, 2 * r + 2), v("emw", 2 * r + 2, 2 * r + 4), SUB)
-        tt(v("tk2", 0, 2), v("tk", 0, 2), v("l16", 0, 2), ADD)
-        if r == ROUNDS - 1:
-            copy(v("tlf", 0, 4, 2), v("tk2", 0, 2))
-        else:
-            copy(v("tl", 2 * r, 2 * r + 2), v("tk2", 0, 2))
+        k = 16 * r
+        tt(v("tk", 0, 2), v("lw", k, k + 2), v("lw", k + 16, k + 18), SUB)
+        for s in range(2):
+            o = v("tlf", 2 * s, 2 * s + 1) if r == ROUNDS - 1 else v("tl", 2 * r + s, 2 * r + s + 1)
+            ts(o, v("tk", s, s + 1), 2.0, MUL, v("l16", s, s + 1), ADD)
 
     def unpack(r):
         for t in range(4):
@@ -323,9 +330,13 @@ def rank_program(g, core, T, topo):
     def lists(r):
         k = 16 * r
         copy(v("clu", 0, 2), v("cnt", 0, 2))
-        ts(v("lim", k + 2, k + 4), v("cnt", 0, 2), float(C), GE, 128.0, MUL)
+        ts(v("lim", k + 6, k + 8), v("cnt", 0, 2), float(C), GE, 128.0, MUL)
         if r < ROUNDS - 1:
-            tt(v("lim", k, k + 2), v("lim", k + 2, k + 4), v("l16", 0, 2), ADD)
+            tt(v("lim", k + 4, k + 6), v("lim", k + 6, k + 8), v("l16", 0, 2), ADD)
+            old = v("nx", 0, 4) if r == 0 else v("lim", k - 16, k - 12)
+            tt(v("lim", k, k + 4), old, v("lim", k + 4, k + 8), MIN)
+        else:
+            tt(v("lim", k + 2, k + 4), v("lim", k - 14, k - 12), v("lim", k + 6, k + 8), MIN)
         flags_out(r)
         for t in range(4):
             act(v("ctl", t, 128, 4), ind(v("zp", 400 * t, 400 * t + 400), v("clu", 0, 2)))
@@ -338,6 +349,14 @@ def rank_program(g, core, T, topo):
     for h in range(7):
         LO.append(LO[h] + 64 * (7 - h))
     qx = pair("qxc", "qxs", 0, 384)
+
+    def state(lo):
+        for b in range(lo, 4):
+            mx(v("pf%d" % b, 0, 384), *pair("ec", "es", 128 * b, 128 * b + 128), *qx)
+
+    def carry(h):
+        ts(v("occ", 4 * h, 4 * h + 4), v("trb", LO[h] + 1, LO[h] + 64, 16), 32.0 * h, ADD)
+
     for r in range(ROUNDS):
         last = r == ROUNDS - 1
         quant(*qx, v("xt", 0, 1536))
@@ -352,33 +371,35 @@ def rank_program(g, core, T, topo):
         quant(*pair("bc", "bs", 0, 128), v("bt", 0, 512))
         mx(v("pe", 0, 128), *pair("bc", "bs", 0, 128), *pair("ctc", "cts", 0, 128))
         if r == 0:
-            quant(*pair("ec", "es", 0, 512), v("et", 0, 2048))
-            mx(v("pf0", 0, 384), *pair("ec", "es", 0, 128), *qx)
+            slots_first()
+            tell()
         else:
-            pack(r - 1)
             flags_in(r - 1)
-        for b in range(1, 4):
-            mx(v("pf%d" % b, 0, 384), *pair("ec", "es", 128 * b, 128 * b + 128), *qx)
-        for b in range(2):
-            act(v("fs", 384 * b, 384 * b + 384), v("pf%d" % b, 0, 384))
+            state(1)
         copy(v("of0", 0, 28), v("pe", 0, 28))
         for h in range(7):
             a, m = LO[h], 7 - h
-            copy(v("res", a, a + 64 * m), ind(v("win", 1024 * h, 1024 * h + 1024), v("of%d" % h, 0, 4 * m)))
+            w, o, b = v("win", 1024 * h, 1024 * h + 1024), "of%d" % h, m - SHARE[h] * (r > 0 or h > 1)
+            if b < m:
+                act(v("res", a + 64 * b, a + 64 * m), ind(w, v(o, 4 * b, 4 * m)))
+            copy(v("res", a, a + 64 * b), ind(w, v(o, 0, 4 * b)))
+            if h % 2:
+                carry(h - 1)
+            if r > 0 and h == 0:
+                pack(r - 1)
             if r == 0 and h == 1:
                 fill(v("fp", 0, 4), 0.0)
                 quant(*pair("qtc", "qts", 0, 128), v("trt", 0, 512))
-            if r == 0 and h == 2:
-                ts(v("obas", 0, 256), v("qrow", 0, 256), v("scl", 0, 1), MUL)
             if r == 0 and h == 3:
-                ts(v("otmp", 0, 256), v("flr", 0, 256), v("scl", 3, 4), MUL, v("scl", 2, 3), ADD)
+                quant(*pair("ec", "es", 0, 512), v("et", 0, 2048))
+                state(0)
+            if h in FSL:
+                t = h - FSL[0]
+                act(v("fs", 384 * t, 384 * t + 384), v("pf%d" % t, 0, 384))
             if h == 5:
-                if r == 0:
-                    tt(v("ow", 0, 256), v("otmp", 0, 256), v("obas", 0, 256), ADD)
-                else:
-                    tt(v("ow", 256 * r, 256 * r + 256), v("ow", 256 * r - 256, 256 * r), v("lrow", 256 * r - 256, 256 * r), MIN)
                 act(v("ores", 0, 384), ind(v("ow", 256 * r, 256 * r + 256), v("occ", 0, 24)))
             if h == 6:
+                turn(v("otr", 0, 384), v("ores", 0, 384))
                 for k in range(4):
                     e = v("otr", 16 * k + 1, 384, 64)
                     run("V", lambda: g.vector.tensor_tensor_scan(T.fp[:, 4 + k:28:4], e[0], e[0], 0.0, MAX, MAX), [v("fp", 4 + k, 28, 4)], [e])
@@ -388,11 +409,9 @@ def rank_program(g, core, T, topo):
                     ts(v("of%d" % (h + 1), k, 4 * (m - 1), 4), v("trb", a + 64 + 16 * k, a + 64 * m, 64), 32.0, MUL, v("trb", a + 16 * k, a + 16 * k + 1), ADD)
             if h == 6:
                 tt(v("lf", 0, 24), v("otr", 0, 384, 16), v("fp", 0, 24), ADD)
+                carry(h)
             if h % 2 == 0:
-                ts(v("occ", 4 * h, 4 * h + 4), v("trb", a + 1, a + 64, 16), 32.0 * h, ADD)
                 ts(v("occ", 4 * h + 4, 4 * h + 8), v("trb", a, a + 64, 16), 32.0 * h + 32.0, ADD)
-            if h == 5:
-                turn(v("otr", 0, 384), v("ores", 0, 384))
         copy(v("lu", 0, 24), v("lf", 0, 24))
         dl = "dl%d" % r
         for lev in range(6):
@@ -419,25 +438,31 @@ def rank_program(g, core, T, topo):
         if last:
             quant(*pair("qvc", "qvs", 0, 128), v("vt", 0, 512))
         ol = v("ol", 0, 24)
-        for t in range(2, 4):
+
+        def pick(t):
             a = 768 * r + 192 * t
             act(v("gt", 384 * (t - 2), 384 * (t - 1)), ind(v("tw", a, a + 128), ol))
-        for t in range(4):
+
+        def diff(t):
             a = 768 * r + 192 * t
             if t < 2:
                 tt(v("zt", t, 1536, 4), ind(v("tw", a, a + 128), ol), v("fs", 384 * t, 384 * t + 384), ADD)
             else:
                 tt(v("zt", t, 1536, 4), v("pf%d" % t, 0, 384), v("gt", 384 * (t - 2), 384 * (t - 1)), ADD)
-        quant(*pair("qzc", "qzs", 0, 384), v("zt", 0, 1536))
-        for s in range(2):
+
+        def mine(s):
             act(v("mm", 384 * s, 384 * s + 384), ind(v("mw", 128 * s, 128 * s + 128), ol))
-        for t in range(4):
-            mx(v("pf%d" % t, 0, 384), *pair("wq", "wp", 128 * t, 128 * t + 128), *pair("qzc", "qzs", 0, 384))
-        for t in range(4):
-            if t < 2:
+
+        def full_size(t, vector):
+            if vector:
                 ts(v("zp", 400 * t, 400 * t + 384), v("zt", t, 1536, 4), 64.0, MUL)
             else:
                 act(v("zp", 400 * t, 400 * t + 384), v("zt", t, 1536, 4), 64.0)
+
+        def products():
+            quant(*pair("qzc", "qzs", 0, 384), v("zt", 0, 1536))
+            for t in range(4):
+                mx(v("pf%d" % t, 0, 384), *pair("wq", "wp", 128 * t, 128 * t + 128), *pair("qzc", "qzs", 0, 384))
 
         def first_of(s):
             e = v("mm", 384 * s, 384 * s + 384)
@@ -450,19 +475,41 @@ def rank_program(g, core, T, topo):
 
         def layer(t):
             tt(v("xt", t, 1536, 4), v("pf%d" % t, 0, 384), v("zp", 400 * t, 400 * t + 384), ADD)
-        first_of(0)
         if last:
+            mine(0)
+            pick(2)
+            pick(3)
+            mine(1)
+            diff(0)
+            diff(1)
+            first_of(0)
+            diff(2)
+            diff(3)
+            full_size(2, False)
+            full_size(3, False)
             first_of(1)
+            full_size(0, True)
+            full_size(1, True)
             lists(r)
-            layer(0)
-            layer(1)
+            products()
             pack(r)
+            for t in range(4):
+                layer(t)
         else:
+            pick(2)
+            pick(3)
+            for t in range(4):
+                diff(t)
+            products()
+            mine(0)
+            mine(1)
+            for t in range(4):
+                full_size(t, t < NZ)
+            first_of(0)
             layer(0)
             first_of(1)
-            layer(1)
-        layer(2)
-        layer(3)
+            for t in range(1, 4):
+                layer(t)
     r = ROUNDS - 1
     quant(*qx, v("xt", 0, 1536))
     mx(v("ps", 0, 384), *pair("qvc", "qvs", 0, 128), *qx)
@@ -471,10 +518,10 @@ def rank_program(g, core, T, topo):
         dma("S", "dout", inp(T.osc[4 * k:4 * k + 4, :]), v("qxs", 0, 384, p=(32 * k, 32 * k + 4)))
     act(v("bpt", 0, 384), ind(v("bw", 0, 128), v("ol", 0, 24)))
     dma("S", "dout", inp(T.bp[:, 0:384]), (T.bpt[0:128:16, :], [("bpt", (0, 128, 0, 384, 1))]))
-    copy(v("yt", 0, 384), v("ps", 0, 384))
+    act(v("yt", 0, 384), v("ps", 0, 384))
     dma("S", "dout", inp(T.y[:]), v("yt", 0, 384))
     take_list(r)
-    ts(v("full", 0, 2), v("emw", 2 * r + 2, 2 * r + 4), 0.0, EQ)
+    ts(v("full", 0, 2), v("lw", 16 * r + 16, 16 * r + 18), 0.0, EQ)
     dma("S", "dout", inp(T.bp[:, 384:416]), v("full", 0, 2))
     unpack(r)
     for t in range(4):

import math
from concourse.bass import DstId, RemoteDMATransfer
from concourse.mybir import dt, AluOpType, AxisListType, ActivationFunctionType

ROUNDS, C = 3, 384
SHARE, FSL, NZ = (3, 3, 2, 2, 1, 1, 0), (3, 4), 1
KIND = {"f": "float32", "b": "bfloat16", "i": "int32", "h": "uint16", "s": "uint8", "c": "float8_e4m3fn_x4"}
SPEC = """b xt 1536 ut 512 vt 512 trt 512 et 2048 ent 2048 ct 512 bt 512 win 7168 tab 64 tat 64 res 1792 trb 1792 ow 768
b ores 512 otr 512 fp 32 lf 32 gt 768 zt 1536 zp 1600 mw 256 mm 768 pr 768 jnk 384 lim 64 ctl 512 zero 512 lw 64 tw 2304
b bw 128 me 4 nx 4
c qxc 384 quc 128 qvc 128 qtc 128 wq 512 ec 512 enc 512 ctc 128 bc 128 qzc 384 qcc0 128 qcc1 128 qcc2 128 lc0 160 lc1 160 lc2 160
s qxs 384 qus 128 qvs 128 qts 128 wp 512 es 512 ens 512 cts 128 bs 128 qzs 384 qcs0 128 qcs1 128 qcs2 128 ls0 160 ls1 160 ls2 160
i tia 32 tib 32 pidx 1 pint 2 flw 2
h occ 32 lu 32 ol 24 clu 2 tl 4 tlf 4 of0 28 of1 28 of2 28 of3 28 of4 28 of5 28 of6 28
f ones 128 idn 128 fs 768 cnt 2 tk 2 rtt 128 yt 384 bpt 384 full 2 pf 2 hrow 7 s16 2 l16 2 i128 128 w5 8 mh 8"""
PSUM = ("ps", "pe", "pf0", "pf1", "pf2", "pf3", "pd0", "pd1")
SCRATCH = {"tdr": ("dram", [160, 32], "bfloat16")}
for _n in ("fo", "fd0", "fd1"):
    SCRATCH[_n] = ("dram", [2, 128, 2], "bfloat16")
for _l in SPEC.split("\n"):
    _w = _l.split()
    for _k in range(1, len(_w), 2):
        SCRATCH[_w[_k]] = ("sbuf", [128, int(_w[_k + 1])], KIND[_w[0]])
for _n in PSUM:
    SCRATCH[_n] = ("psum", [128, 512], "float32")
DMAS = "dx du dti dtr dw dfl dfo dow0 dv dw0 dw1 dtd dw2 dw4 dl0 dl1 dl2 dlr0 dlr1 dlw0 dlw1 dout".split()
SEMAPHORES = "cv ca ct_ cp loc rn rf0 rf1 rf2 rc0 rc1 rc2 rs0 rs1 rs2".split() + DMAS

ADD, SUB, MUL, MAX, MIN = AluOpType.add, AluOpType.subtract, AluOpType.mult, AluOpType.max, AluOpType.min
EQ, NE, GT, GE = AluOpType.is_equal, AluOpType.not_equal, AluOpType.is_gt, AluOpType.is_ge
COPY = ActivationFunctionType.Copy


def rank_program(g, core, T, topo):
    rank = T.rank_of(core)
    if rank is None:
        return
    nxt, prv = T.cores[(rank + 1) % len(T.cores)], T.cores[(rank - 1) % len(T.cores)]
    eng = {"V": g.vector, "A": g.scalar, "T": g.tensor, "S": g.sync, "P": g}
    semof = {"V": "cv", "A": "ca", "T": "ct_", "P": "cp"}
    total = {}
    known = {q: {} for q in eng}
    clock = {}
    wr, rd = {}, {}

    def hit(a, b):
        return a[0] < b[1] and b[0] < a[1] and a[2] < b[3] and b[2] < a[3] and (a[2] - b[2]) % math.gcd(a[4], b[4]) == 0

    def covers(a, b):
        return a[4] == 1 and a[0] <= b[0] and b[1] <= a[1] and a[2] <= b[2] and b[3] <= a[3]

    def learn(q, sem, val):
        k = known[q]
        if k.get(sem, 0) >= val:
            return
        if sem in DMAS:
            val = total[sem]
        eng[q].wait_ge(T.sem[sem], val)
        k[sem] = val
        for (s, x), c in clock.items():
            if s == sem and x <= val and (sem in DMAS or x == val):
                for s2, x2 in c.items():
                    if k.get(s2, 0) < x2:
                        k[s2] = x2

    def need(q, outs, ins):
        toks = {}

        def add(e):
            toks[e[2]] = max(toks.get(e[2], 0), e[3])
        for name, reg in ins:
            for e in wr.get(name, []):
                if hit(reg, e[0]):
                    add(e)
            if name in PSUM:
                for e in rd.get(name, []):
                    if e[1] != q:
                        add(e)
        for name, reg in outs:
            for e in wr.get(name, []) + rd.get(name, []):
                if name in PSUM or hit(reg, e[0]):
                    add(e)
        for s in sorted(toks):
            learn(q, s, toks[s])

    def note(q, outs, ins, sem, val):
        for name, reg in outs:
            wr[name] = [e for e in wr.get(name, []) if not covers(reg, e[0])] + [(reg, q, sem, val)]
            rd[name] = [e for e in rd.get(name, []) if not covers(reg, e[0])]
        for name, reg in ins:
            rd.setdefault(name, []).append((reg, q, sem, val))

    def regs(vs):
        out = []
        for e in vs:
            out += e[1]
        return out

    def run(q, fn, outs, ins):
        o, i = regs(outs), regs(ins)
        need(q, o, i)
        sem = semof[q]
        total[sem] = total.get(sem, 0) + 1
        clock[(sem, total[sem])] = dict(known[q])
        fn().then_inc(T.sem[sem], 1)
        note(q, o, i, sem, total[sem])

    def dma(q, sem, out, in_):
        o, i = regs([out]), regs([in_])
        need(q, o, i)
        total[sem] = total.get(sem, 0) + 16
        clock[(sem, total[sem])] = dict(known[q])
        eng[q].dma_start(out[0], in_[0]).then_inc(T.sem[sem], 16)
        note(q, o, i, sem, total[sem])

    def v(name, a, b, s=1, p=(0, 128)):
        t = T[name]
        return (t[p[0]:p[1], a:b:s] if s != 1 else t[p[0]:p[1], a:b], [(name, (p[0], p[1], a, b, s))])

    def codes(name, a, b):
        return (T[name][:, a:b].bitcast(dt.uint8), [(name, (0, 128, a, b, 1))])

    def rows(name, a, b):
        return (T[name][a:b, :], [(name, (a, b, 0, 32, 1))])

    def slot(name, k=None):
        return (T[name][:], [(name, (0, 2, 0, 256, 1))]) if k is None else (T[name][k], [(name, (k, k + 1, 0, 256, 1))])

    def inp(ap):
        return (ap, [])

    def ind(win, off):
        return (win[0].indirect(off[0]), win[1] + off[1])

    def copy(out, in_):
        run("V", lambda: g.vector.tensor_copy(out[0], in_[0]), [out], [in_])

    def act(out, in_, scale=1.0):
        run("A", lambda: g.scalar.activation(out[0], in_[0], COPY, scale=scale) if scale != 1.0 else g.scalar.activation(out[0], in_[0], COPY), [out], [in_])

    def tt(out, a, b, op):
        run("V", lambda: g.vector.tensor_tensor(out[0], a[0], b[0], op), [out], [a, b])

    def ts(out, a, s1, op0, s2=None, op1=None):
        ins = [a] + [s for s in (s1, s2) if isinstance(s, tuple)]
        x1 = s1[0] if isinstance(s1, tuple) else s1
        x2 = s2[0] if isinstance(s2, tuple) else s2
        if op1 is None:
            run("V", lambda: g.vector.tensor_scalar(out[0], a[0], x1, None, op0), [out], ins)
        else:
            run("V", lambda: g.vector.tensor_scalar(out[0], a[0], x1, x2, op0, op1), [out], ins)

    def fill(out, c):
        run("V", lambda: g.vector.memset(out[0], c), [out], [])

    def quant(c, s, in_):
        run("V", lambda: g.vector.quantize_mx(c[0], s[0], in_[0]), [c, s], [in_])

    def mx(out, lc, ls, rc, rs):
        run("T", lambda: g.tensor.matmul_mx(out[0], lc[0], ls[0], rc[0], rs[0], True, True), [out], [lc, ls, rc, rs])

    def pair(c, s, a, b):
        return v(c, a, b), v(s, a, b)

    def turn(out, in_):
        run("V", lambda: g.vector.transpose(out[0], in_[0]), [out], [in_])

    def iota(out, pattern, base, cm):
        run("P", lambda: g.iota(out[0], pattern, base, cm, allow_small_or_imprecise_dtypes=True), [out], [])

    def one(G, k=1):
        return (16 * G, 16 * G + k)

    dma("S", "dti", v("tia", 0, 32), inp(T.ti[0:4, :]))
    dma("A", "dti", v("tib", 0, 32, p=(0, 96)), inp(T.ti[4:7, :]))
    dma("S", "dx", v("xt", 0, 1536), inp(T.x[:]))
    dma("A", "du", v("ut", 0, 512), inp(T.u[:]))
    dma("S", "dtr", v("trt", 0, 128), inp(T.tr[:]))
    dma("S", "dfl", v("flw", 0, 2), inp(T.fl[:]))

    fill(v("ones", 0, 128), 1.0)
    iota(v("pidx", 0, 1), [[0, 1]], 0, 1)
    run("P", lambda: g.affine_select(T.idn[:], T.ones[:], [[-1, 128]], EQ, 0.0, 0, 1), [v("idn", 0, 128)], [v("ones", 0, 128)])
    iota(v("hrow", 0, 7), [[1, 7]], 1, 0)
    iota(v("s16", 0, 2), [[16, 2]], 0, 0)
    iota(v("win", 0, 1024), [[1, 32], [0, 32]], 0, 0)
    iota(v("win", 2048, 3072), [[0, 32], [1, 32]], 0, 0)
    iota(v("win", 6144, 7168), [[0, 32], [1, 32]], 0, 0)
    iota(v("i128", 0, 128), [[1, 128]], -32, 0)
    iota(v("ow", 0, 768), [[0, 768]], 0, 0)
    iota(v("tw", 0, 2304), [[0, 2304]], 0, 0)
    iota(v("bw", 0, 64), [[0, 2], [1, 2], [2, 16]], 0, 0)
    fill(v("ent", 0, 2048), 0.0)
    for b in range(4):
        ts(v("ent", 512 * b + b, 512 * b + 512, 4), v("idn", 0, 128), -(2.0 ** -6), MUL)
    fill(v("win", 1024, 2048), 0.0)
    fill(v("ct", 0, 512), 0.0)
    run("V", lambda: g.vector.tensor_scalar(T.pint[:, 0:1], T.pidx[:], 15, None, AluOpType.bitwise_and), [v("pint", 0, 1)], [v("pidx", 0, 1)])
    run("V", lambda: g.vector.tensor_scalar(T.pint[:, 1:2], T.pidx[:], 4, None, AluOpType.arith_shift_right), [v("pint", 1, 2)], [v("pidx", 0, 1)])
    copy(v("pf", 0, 2), v("pint", 0, 2))
    i15, grp = v("pf", 0, 1), v("pf", 1, 2)
    for k in range(5):
        ts(v("w5", k, k + 1), i15, float(k), EQ, 2.0 ** (4 - k), MUL)
    ts(v("w5", 6, 7), grp, 0.0, EQ, 32.0, MUL)
    run("V", lambda: g.vector.tensor_reduce(T.w5[:, 5:6], T.w5[:, 0:5], AxisListType.X, ADD), [v("w5", 5, 6)], [v("w5", 0, 5)])
    wcol = v("w5", 5, 6)
    fill(v("bt", 384, 512), 0.0)
    fill(v("trt", 128, 512), 0.0)
    tt(v("w5", 7, 8), v("w5", 6, 7), wcol, MUL)
    ts(v("mh", 0, 7), v("hrow", 0, 7), grp, EQ, wcol, MUL)
    ts(v("l16", 0, 2), v("s16", 0, 2), i15, ADD)
    for k in range(4):
        ts(v("ct", 5 * k, 112, 16), v("mh", 0, 7), v("w5", 7, 8), ADD)
    copy(v("tab", 0, 32), v("tia", 0, 32))
    copy(v("tab", 32, 64, p=(0, 96)), v("tib", 0, 32, p=(0, 96)))
    turn(v("tat", 0, 32), v("tab", 0, 32))
    turn(v("tat", 32, 64, p=(0, 96)), v("tab", 32, 64, p=(0, 96)))
    act(v("win", 3072, 4096), v("ent", 0, 1024), 0.0)
    for G in range(6):
        dma("SA"[G % 2], "dw0", v("win", 0, 1024, p=one(G)), v("tab", 0, 32, p=(0, 32)))
    dma("S", "dtd", rows("tdr", 0, 64), v("tat", 0, 32, p=(64, 128)))
    dma("A", "dtd", rows("tdr", 64, 160), v("tat", 32, 64, p=(0, 96)))
    for G in range(6):
        dma("SA"[G % 2], "dw1", v("win", 1024, 2048, p=one(G)), v("tat", 0, 32, p=(32, 64)))
    act(v("win", 5120, 6144), v("ent", 0, 1024), 0.0)
    act(v("win", 4096, 5120), v("win", 2048, 3072))
    act(v("et", 0, 2048), v("ent", 0, 2048), -1.0)
    for G in range(6):
        dma("S", "dw2", v("win", 2048, 4096, p=one(G)), rows("tdr", 0, 64))
    for G in range(6):
        dma("S", "dw4", v("win", 4096, 7168, p=one(G)), rows("tdr", 64, 160))
    dma("S", "dw", codes("wq", 0, 512), inp(T.wc[:]))
    dma("S", "dw", v("wp", 0, 512), inp(T.ws[:]))
    dma("S", "dv", v("vt", 0, 512), inp(T.v[:]))
    quant(*pair("ctc", "cts", 0, 128), v("ct", 0, 512))
    quant(*pair("quc", "qus", 0, 128), v("ut", 0, 512))

    def slots_first():
        ts(v("me", 2, 4), v("flw", 0, 2), -64.0, MUL, 64.0, ADD)
        ts(v("tk", 0, 2), v("flw", 0, 2), -32.0, MUL, 32.0, ADD)
        tt(v("me", 0, 2), v("tk", 0, 2), v("l16", 0, 2), ADD)
        for k in range(2):
            dma("S", "dfo", slot("fo", k), v("me", 2 * k, 2 * k + 2))
        for G in range(6):
            dma("S", "dow0", v("ow", 0, 256, p=one(G, 2)), slot("fo"))
        copy(v("lw", 0, 2), v("me", 2, 4))

    def first_rest():
        for s in range(2):
            ts(v("mw", 128 * s, 128 * s + 128), v("i128", 0, 128), v("l16", s, s + 1), NE)
        fill(v("bw", 64, 128), -1.0)
        for t in range(4):
            fill(v("zp", 400 * t + 384, 400 * t + 400), 0.0)
        fill(v("ctl", 128, 512), 0.0)
        fill(v("zero", 0, 512), 0.0)
        for k in range(3):
            quant(*pair("lc%d" % k, "ls%d" % k, 32, 160), v("zero", 0, 512))

    elist = topo.engines(core, nxt)
    n = 1
    while n * 2 <= len(elist) and n < 8:
        n *= 2
    elist = elist[:n]
    full_mask = sum(1 << e for e in elist)
    half = len(elist) // 2
    halves = [sum(1 << e for e in elist[:half]), sum(1 << e for e in elist[half:])]
    rid, pid, _ = topo.addr(nxt)

    def send(ins, cnt, fn):
        need("P", [], regs(ins))
        total["loc"] = total.get("loc", 0) + cnt
        fn()
        note("P", [], regs(ins), "loc", total["loc"])

    def arrived(where, sem, cnt=n):
        total[sem] = cnt
        note("R", where, [], sem, cnt)

    def tell():
        ridb, pidb, _b = topo.addr(prv)
        maskb = sum(1 << e for e in topo.engines(core, prv)[:half])
        send([v("me", 0, 4)], half, lambda: g.remote_dma(T.nx[:], T.me[:], T.sem.rn, T.sem.loc, pidb, ridb, maskb))
        arrived([("nx", (0, 128, 0, 4, 1))], "rn", half)

    def flags_out(r):
        k, sem = 16 * r, "rf%d" % r
        if r == ROUNDS - 1:
            send([v("lim", k + 2, k + 4)], n, lambda: g.remote_dma(T.lw[:, k + 16:k + 18], T.lim[:, k + 2:k + 4], T.sem[sem], T.sem.loc, pid, rid, full_mask))
            arrived([("lw", (0, 128, k + 16, k + 18, 1))], sem)
        else:
            fd = T["fd%d" % r]
            tr = [RemoteDMATransfer(dst_ids=[DstId(rid=rid, pnc=pid)], dma_engine_mask=halves[e], remote_sem=T.sem[sem], src=T.lim[:, k + 2 * e:k + 2 * e + 2], dst=fd[e]) for e in range(2)]
            send([v("lim", k, k + 4)], n, lambda: g.remote_dma_fused(tr, local_sem=T.sem.loc))
            arrived([("fd%d" % r, (0, 2, 0, 256, 1))], sem)

    def claims_out(r):
        lc, ls, qc, qs = T["lc%d" % r], T["ls%d" % r], T["qcc%d" % r], T["qcs%d" % r]
        send([v("qcc%d" % r, 0, 32)], n, lambda: g.remote_dma(lc[:, 0:32].bitcast(dt.uint8), qc[:, 0:32].bitcast(dt.uint8), T.sem["rc%d" % r], T.sem.loc, pid, rid, full_mask))
        send([v("qcs%d" % r, 0, 32)], n, lambda: g.remote_dma(ls[:, 0:32], qs[:, 0:32], T.sem["rs%d" % r], T.sem.loc, pid, rid, full_mask))
        arrived([("lc%d" % r, (0, 128, 0, 32, 1))], "rc%d" % r)
        arrived([("ls%d" % r, (0, 128, 0, 32, 1))], "rs%d" % r)

    def flags_in(r):
        for G in range(6):
            dma("S", "dlr%d" % r, v("ow", 256 * r + 256, 256 * r + 512, p=one(G, 2)), slot("fd%d" % r))
        dma("S", "dlw%d" % r, v("lw", 16 * r + 16, 16 * r + 18), slot("fd%d" % r, 1))

    def take_list(r):
        k = 16 * r
        tt(v("tk", 0, 2), v("lw", k, k + 2), v("lw", k + 16, k + 18), SUB)
        for s in range(2):
            o = v("tlf", 2 * s, 2 * s + 1) if r == ROUNDS - 1 else v("tl", 2 * r + s, 2 * r + s + 1)
            ts(o, v("tk", s, s + 1), 2.0, MUL, v("l16", s, s + 1), ADD)

    def unpack(r):
        for t in range(4):
            pd = "pd%d" % (t % 2)
            mx(v(pd, 0, 128), *pair("enc", "ens", 128 * t, 128 * t + 128), *pair("lc%d" % r, "ls%d" % r, 0, 128))
            a = 768 * r + 192 * t + 128
            if t % 2 and r == ROUNDS - 1:
                copy(v("tw", a, a + 32), v(pd, 0, 32))
            else:
                act(v("tw", a, a + 32), v(pd, 0, 32))

    def new_slots(r):
        for t in range(4):
            a = 768 * r + 192 * t
            act(v("tw", a + 768, a + 800), ind(v("tw", a, a + 160), v("tl", 2 * r, 2 * r + 2)))

    def lists(r):
        k = 16 * r
        copy(v("clu", 0, 2), v("cnt", 0, 2))
        ts(v("lim", k + 6, k + 8), v("cnt", 0, 2), float(C), GE, 128.0, MUL)
        if r < ROUNDS - 1:
            tt(v("lim", k + 4, k + 6), v("lim", k + 6, k + 8), v("l16", 0, 2), ADD)
            old = v("nx", 0, 4) if r == 0 else v("lim", k - 16, k - 12)
            tt(v("lim", k, k + 4), old, v("lim", k + 4, k + 8), MIN)
        else:
            tt(v("lim", k + 2, k + 4), v("lim", k - 14, k - 12), v("lim", k + 6, k + 8), MIN)
        flags_out(r)
        for t in range(4):
            act(v("ctl", t, 128, 4), ind(v("zp", 400 * t, 400 * t + 400), v("clu", 0, 2)))

    def pack(r):
        quant(*pair("qcc%d" % r, "qcs%d" % r, 0, 128), v("ctl", 0, 512))
        claims_out(r)

    LO = [0]
    for h in range(7):
        LO.append(LO[h] + 64 * (7 - h))
    qx = pair("qxc", "qxs", 0, 384)

    def state(lo):
        for b in range(lo, 4):
            mx(v("pf%d" % b, 0, 384), *pair("ec", "es", 128 * b, 128 * b + 128), *qx)

    def carry(h):
        ts(v("occ", 4 * h, 4 * h + 4), v("trb", LO[h] + 1, LO[h] + 64, 16), 32.0 * h, ADD)

    for r in range(ROUNDS):
        last = r == ROUNDS - 1
        quant(*qx, v("xt", 0, 1536))
        mx(v("ps", 0, 384), *pair("quc", "qus", 0, 128), *qx)
        if r > 0:
            mx(v("pf0", 0, 384), *pair("ec", "es", 0, 128), *qx)
            lists(r - 1)
        else:
            quant(*pair("enc", "ens", 0, 512), v("ent", 0, 2048))
        for x in range(16):
            ts(v("bt", 24 * x, 24 * x + 24), v("ps", x, 384, 16), 0.0, GT)
        quant(*pair("bc", "bs", 0, 128), v("bt", 0, 512))
        mx(v("pe", 0, 128), *pair("bc", "bs", 0, 128), *pair("ctc", "cts", 0, 128))
        if r == 0:
            slots_first()
            tell()
        else:
            flags_in(r - 1)
            state(1)
        copy(v("of0", 0, 28), v("pe", 0, 28))
        for h in range(7):
            a, m = LO[h], 7 - h
            w, o, b = v("win", 1024 * h, 1024 * h + 1024), "of%d" % h, m - SHARE[h] * (r > 0 or h > 1)
            if b < m:
                act(v("res", a + 64 * b, a + 64 * m), ind(w, v(o, 4 * b, 4 * m)))
            copy(v("res", a, a + 64 * b), ind(w, v(o, 0, 4 * b)))
            if h % 2:
                carry(h - 1)
            if r > 0 and h == 0:
                pack(r - 1)
            if r == 0 and h == 1:
                fill(v("fp", 0, 4), 0.0)
                quant(*pair("qtc", "qts", 0, 128), v("trt", 0, 512))
            if r == 0 and h == 3:
                quant(*pair("ec", "es", 0, 512), v("et", 0, 2048))
                state(0)
            if h in FSL:
                t = h - FSL[0]
                act(v("fs", 384 * t, 384 * t + 384), v("pf%d" % t, 0, 384))
            if h == 5:
                act(v("ores", 0, 384), ind(v("ow", 256 * r, 256 * r + 256), v("occ", 0, 24)))
            if h == 6:
                turn(v("otr", 0, 384), v("ores", 0, 384))
                for k in range(4):
                    e = v("otr", 16 * k + 1, 384, 64)
                    run("V", lambda: g.vector.tensor_tensor_scan(T.fp[:, 4 + k:28:4], e[0], e[0], 0.0, MAX, MAX), [v("fp", 4 + k, 28, 4)], [e])
            turn(v("trb", a, a + 64 * m), v("res", a, a + 64 * m))
            if h < 6:
                for k in range(4):
                    ts(v("of%d" % (h + 1), k, 4 * (m - 1), 4), v("trb", a + 64 + 16 * k, a + 64 * m, 64), 32.0, MUL, v("trb", a + 16 * k, a + 16 * k + 1), ADD)
            if h == 6:
                tt(v("lf", 0, 24), v("otr", 0, 384, 16), v("fp", 0, 24), ADD)
                carry(h)
            if h % 2 == 0:
                ts(v("occ", 4 * h + 4, 4 * h + 8), v("trb", a, a + 64, 16), 32.0 * h + 32.0, ADD)
        copy(v("lu", 0, 24), v("lf", 0, 24))
        dl = "dl%d" % r
        for lev in range(6):
            dma("S", dl, v("ol", 0, 24, p=one(lev, 16)), v("lu", 4 * lev, 4 * lev + 4, p=(0, 96)))
        if r == 0:
            for t in range(4):
                pd = "pd%d" % (t % 2)
                mx(v(pd, 0, 128), *pair("enc", "ens", 128 * t, 128 * t + 128), *pair("qtc", "qts", 0, 128))
                for s in range(2):
                    act(v("tw", 192 * t + 16 * s, 192 * t + 16 * s + 16), v(pd, s, 32, 2))
        copy(v("ores", 384, 512), ind(v("ow", 256 * r, 256 * r + 256), v("occ", 24, 32)))
        turn(v("otr", 384, 512), v("ores", 384, 512))
        tt(v("fp", 28, 32), v("fp", 24, 28), v("otr", 385, 448, 16), MAX)
        tt(v("lf", 24, 32), v("otr", 384, 512, 16), v("fp", 24, 32), ADD)
        copy(v("lu", 24, 32), v("lf", 24, 32))
        dma("S", dl, v("ol", 0, 24, p=one(6, 16)), v("lu", 24, 28, p=(0, 96)))
        dma("A", dl, v("ol", 0, 24, p=one(7, 16)), v("lu", 28, 32, p=(0, 96)))
        if r == 0:
            first_rest()
        else:
            unpack(r - 1)
            take_list(r - 1)
            new_slots(r - 1)
        if last:
            quant(*pair("qvc", "qvs", 0, 128), v("vt", 0, 512))
        ol = v("ol", 0, 24)

        def pick(t):
            a = 768 * r + 192 * t
            act(v("gt", 384 * (t - 2), 384 * (t - 1)), ind(v("tw", a, a + 128), ol))

        def diff(t):
            a = 768 * r + 192 * t
            if t < 2:
                tt(v("zt", t, 1536, 4), ind(v("tw", a, a + 128), ol), v("fs", 384 * t, 384 * t + 384), ADD)
            else:
                tt(v("zt", t, 1536, 4), v("pf%d" % t, 0, 384), v("gt", 384 * (t - 2), 384 * (t - 1)), ADD)

        def mine(s):
            act(v("mm", 384 * s, 384 * s + 384), ind(v("mw", 128 * s, 128 * s + 128), ol))

        def full_size(t, vector):
            if vector:
                ts(v("zp", 400 * t, 400 * t + 384), v("zt", t, 1536, 4), 64.0, MUL)
            else:
                act(v("zp", 400 * t, 400 * t + 384), v("zt", t, 1536, 4), 64.0)

        def products():
            quant(*pair("qzc", "qzs", 0, 384), v("zt", 0, 1536))
            for t in range(4):
                mx(v("pf%d" % t, 0, 384), *pair("wq", "wp", 128 * t, 128 * t + 128), *pair("qzc", "qzs", 0, 384))

        def first_of(s):
            e = v("mm", 384 * s, 384 * s + 384)
            o = v("pr", 384 * s, 384 * s + 384)
            run("V", lambda: g.vector.tensor_tensor_scan(o[0], e[0], e[0], 1.0, MUL, MIN), [o], [e])
            if last:
                run("V", lambda: g.vector.tensor_reduce(T.cnt[:, s:s + 1], o[0], AxisListType.X, ADD), [v("cnt", s, s + 1)], [o])
            else:
                run("A", lambda: g.scalar.activation(T.jnk[:], o[0], COPY, accum_out=T.cnt[:, s:s + 1]), [v("jnk", 0, 384), v("cnt", s, s + 1)], [o])

        def layer(t):
            tt(v("xt", t, 1536, 4), v("pf%d" % t, 0, 384), v("zp", 400 * t, 400 * t + 384), ADD)
        if last:
            mine(0)
            pick(2)
            pick(3)
            mine(1)
            diff(0)
            diff(1)
            first_of(0)
            diff(2)
            diff(3)
            full_size(2, False)
            full_size(3, False)
            first_of(1)
            full_size(0, True)
            full_size(1, True)
            lists(r)
            products()
            pack(r)
            for t in range(4):
                layer(t)
        else:
            pick(2)
            pick(3)
            for t in range(4):
                diff(t)
            products()
            mine(0)
            mine(1)
            for t in range(4):
                full_size(t, t < NZ)
            first_of(0)
            layer(0)
            first_of(1)
            for t in range(1, 4):
                layer(t)
    r = ROUNDS - 1
    quant(*qx, v("xt", 0, 1536))
    mx(v("ps", 0, 384), *pair("qvc", "qvs", 0, 128), *qx)
    dma("S", "dout", inp(T.oc[:]), codes("qxc", 0, 384))
    for k in range(4):
        dma("S", "dout", inp(T.osc[4 * k:4 * k + 4, :]), v("qxs", 0, 384, p=(32 * k, 32 * k + 4)))
    act(v("bpt", 0, 384), ind(v("bw", 0, 128), v("ol", 0, 24)))
    dma("S", "dout", inp(T.bp[:, 0:384]), (T.bpt[0:128:16, :], [("bpt", (0, 128, 0, 384, 1))]))
    act(v("yt", 0, 384), v("ps", 0, 384))
    dma("S", "dout", inp(T.y[:]), v("yt", 0, 384))
    take_list(r)
    ts(v("full", 0, 2), v("lw", 16 * r + 16, 16 * r + 18), 0.0, EQ)
    dma("S", "dout", inp(T.bp[:, 384:416]), v("full", 0, 2))
    unpack(r)
    for t in range(4):
        a = 768 * r + 192 * t
        for s in range(2):
            out, win = v("rtt", 4 * s + t, 128, 8), ind(v("tw", a, a + 160), v("tlf", 2 * s, 2 * s + 1))
            if t % 2:
                ts(out, win, -64.0, MUL)
            else:
                act(out, win, -64.0)
    dma("S", "dout", inp(T.rt[:]), v("rtt", 0, 128))
    for s in sorted(total):
        if known["P"].get(s, 0) < total[s]:
            g.wait_ge(T.sem[s], total[s])
